import numpy as np
import ml_dtypes


def mxq(x, axis, fmt="e4m3"):
    dtype, down = {"e4m3": (ml_dtypes.float8_e4m3fn, 7), "e5m2": (ml_dtypes.float8_e5m2, 14)}[fmt]
    v = np.moveaxis(np.asarray(x, np.float32).astype(ml_dtypes.bfloat16).astype(np.float64), axis, -1)
    blocks = v.reshape(v.shape[:-1] + (-1, 32))
    amax = np.abs(blocks).max(-1, keepdims=True)
    byte = np.maximum(np.where(amax > 0, np.frexp(amax)[1] - 1 + 127, 0) - down, 1)
    scale = np.exp2(byte - 127.0)
    codes = (blocks / scale).astype(np.float32).astype(dtype).astype(np.float64)
    return np.moveaxis((codes * scale).reshape(v.shape), -1, axis)


WIDE = False


def mx_kscale(k):
    if not WIDE:
        return np.ones(k)
    levels = np.array([10, -10, 5, -5, 0])
    if k % 512:
        return np.exp2(np.random.permutation(np.resize(levels, k // 32))).repeat(32)
    a = np.empty((k // 512, 16))
    for p in range(k // 512):
        a[p, :8] = np.random.permutation(np.resize(levels, 8))
        for g in range(8):
            far = levels[np.abs(levels - a[p, g]) >= 10]
            a[p, g + 8] = far[np.random.randint(len(far))]
    return np.exp2(a.ravel()).repeat(32)


BF16 = ml_dtypes.bfloat16


def bf(x):
    return np.asarray(x, np.float32).astype(BF16)


def f64(x):
    return np.asarray(x).astype(np.float64)


E2M1 = np.array([0.0, 0.5, 1.0, 1.5, 2.0, 3.0, 4.0, 6.0, -0.0, -0.5, -1.0, -1.5, -2.0, -3.0, -4.0, -6.0])


def pack_weight(w, fmt):
    k, n = w.shape
    w = f64(bf(w)).reshape(k // 32, 32, n)
    amax = np.abs(w).max(1)
    if fmt == "e4m3":
        byte = np.frexp(amax)[1] - 1 + 127 - 7
    else:
        mant, ex = np.frexp(amax / 6.0)
        byte = np.where(mant > 0.5, ex, ex - 1) + 127
    byte = np.clip(np.where(amax > 0, byte, 1), 1, 254)
    scaled = (w * np.exp2(127.0 - byte)[:, None, :]).reshape(k, n).astype(np.float32)
    by_word = np.ascontiguousarray(scaled.reshape(k // 512, 128, 4, n).transpose(0, 1, 3, 2))
    if fmt == "e4m3":
        words = by_word.astype(ml_dtypes.float8_e4m3fn).view(np.uint8)
    else:
        c = by_word.astype(ml_dtypes.float4_e2m1fn).view(np.uint8) & 0xF
        words = c[..., 0::2] | (c[..., 1::2] << 4)
    return np.ascontiguousarray(words), np.ascontiguousarray(byte.astype(np.uint8).reshape(k // 512, 16, n))


def unpack_weight(words, scales, fmt):
    g, p, n, _ = words.shape
    if fmt == "e4m3":
        vals = np.ascontiguousarray(words).view(ml_dtypes.float8_e4m3fn).astype(np.float64)
    else:
        nib = np.empty((g, p, n, 4), np.uint8)
        nib[..., 0::2] = words & 0xF
        nib[..., 1::2] = words >> 4
        vals = E2M1[nib]
    vals = vals * np.repeat(np.exp2(scales.astype(np.float64) - 127.0), 8, axis=1)[..., None]
    return vals.transpose(0, 1, 3, 2).reshape(g * 512, n)
def pack4(w):
    words, scales = pack_weight(w, "e2m1")
    return words.reshape(words.shape[0], 128, -1), scales


def unpack4(words, scales):
    return unpack_weight(words.reshape(words.shape[0], 128, -1, 2), scales, "e2m1")


M, K, G, J, R = 2048, 1024, 512, 4, 1024


def setup_inputs():
    s, u = mx_kscale(K), mx_kscale(M)
    amp = np.exp(0.3 * np.random.standard_normal(M))
    a = np.random.standard_normal((M, K)) * amp[:, None]
    f = np.random.standard_normal((K, G * J)) / np.sqrt(K)
    cap = 1.0 + 0.2 * np.abs(np.random.standard_normal(M))
    d = np.random.standard_normal((M, R)) / np.sqrt(M)
    d_words, d_scales = pack4(d / (u * u)[:, None])
    return {"a": bf(a * s * u[:, None]),
            "f": bf(f / s[:, None]),
            "cap": bf(cap * u * u),
            "d_words": d_words,
            "d_scales": d_scales}


def reference(a, f, cap, d_words, d_scales):
    d = unpack4(d_words, d_scales)
    w = mxq(f64(a), 1, "e4m3") @ mxq(f64(f), 0, "e4m3")
    e = np.square(w).reshape(M, G, J).mean(axis=2)
    h = np.minimum(e, f64(cap)[:, None])
    return d.T @ mxq(h, 0, "e4m3")

@@ -1,0 +1,305 @@
+from contextlib import ExitStack
+
+import concourse.mybir as mybir
+from concourse.masks import make_identity
+
+F32 = mybir.dt.float32
+BF16 = mybir.dt.bfloat16
+U32 = mybir.dt.uint32
+I32 = mybir.dt.int32
+U8 = mybir.dt.uint8
+FP8X4 = mybir.dt.float8_e4m3fn_x4
+FP4X4 = mybir.dt.float4_e2m1fn_x4
+SQUARE = mybir.ActivationFunctionType.Square
+ADD = mybir.AluOpType.add
+MIN = mybir.AluOpType.min
+
+M, K, N, G, R = 2048, 1024, 2048, 512, 1024
+FLOPS = 2 * M * K * N + 2 * R * M * G
+
+P = 128
+CHUNKS = 4
+GROUPS = 4
+TILES = 4
+PASSES = 2
+UNITS = CHUNKS * GROUPS
+F_SCALAR_COLUMNS = (192, 64, 256, 256)
+
+
+def tile_capped_leverage_design_totals_s13_kernel(tc, a, f, cap, d_words, d_scales, out):
+    nc = tc.nc
+    with ExitStack() as ctx:
+        keep = ctx.enter_context(tc.tile_pool(name="keep", bufs=1))
+        stage = ctx.enter_context(tc.tile_pool(name="stage", bufs=2))
+        psum = ctx.enter_context(tc.psum_pool(name="psum", bufs=2))
+
+        ident = keep.tile([P, P], F32, align_bytes=64)
+        a_raw = keep.tile([P, GROUPS, TILES, K], BF16, align_bytes=64)
+        a_codes = keep.tile([P, GROUPS, 1024], U32, align_bytes=64)
+        a_scales = keep.tile([P, GROUPS, 1024], U8, align_bytes=64)
+        f_raw = keep.tile([P, CHUNKS, PASSES, 4, 512], BF16, align_bytes=64)
+        f_codes = keep.tile([P, CHUNKS, 1024], U32, align_bytes=64)
+        f_scales = keep.tile([P, CHUNKS, 1024], U8, align_bytes=64)
+        h_codes = keep.tile([P, CHUNKS, 512], U32, align_bytes=64)
+        h_scales = keep.tile([P, CHUNKS, 512], U8, align_bytes=64)
+        dw = keep.tile([P, GROUPS, 2 * R], U8, align_bytes=64)
+        dsc = keep.tile([P, GROUPS, R], U8, align_bytes=64)
+        cap_sb = keep.tile([P, GROUPS, TILES], BF16, align_bytes=64)
+        warm = keep.tile([P, 2], F32, align_bytes=64)
+
+        ctx.enter_context(tc.manual_schedule())
+
+        def load_a(g, t0, t1):
+            src = a[512 * g : 512 * (g + 1), :].rearrange("(m t) k -> m t k", t=TILES)
+            nc.sync.dma_start(out=a_raw[:, g, t0:t1, :], in_=src[:, t0:t1, :])
+
+        def load_f(c, h):
+            src = f[512 * h : 512 * (h + 1), 512 * c : 512 * (c + 1)]
+            nc.sync.dma_start(out=f_raw[:, c, h, :, :], in_=src.rearrange("(p j) w -> p j w", j=4))
+
+        load_a(0, 0, 1)
+        load_f(0, 0)
+        load_f(0, 1)
+        load_a(0, 1, 2)
+        load_a(0, 2, 4)
+        load_a(1, 0, 4)
+        load_f(1, 0)
+        load_a(2, 0, 4)
+        load_f(1, 1)
+        load_a(3, 0, 4)
+        for c in (2, 3):
+            for h in range(PASSES):
+                load_f(c, h)
+        nc.sync.dma_start(out=dw[:].bitcast(I32), in_=d_words.rearrange("g p n -> p g n").bitcast(I32))
+        nc.scalar.dma_start(out=cap_sb[:], in_=cap.rearrange("(g p t) -> p g t", g=GROUPS, t=TILES))
+
+        make_identity(nc, ident[:])
+        nc.gpsimd.memset(dsc[:].bitcast(I32), 0)
+        for q in range(4):
+            nc.sync.dma_start(
+                out=dsc[32 * q : 32 * q + 4, :, :].bitcast(I32),
+                in_=d_scales[:, 4 * q : 4 * q + 4, :].rearrange("g r n -> r g n").bitcast(I32),
+            )
+        nc.vector.memset(warm[:, 0:1], 0.0)
+        nc.scalar.activation(out=warm[:, 1:2], in_=warm[:, 0:1], func=SQUARE)
+
+        def transpose_a(g, t):
+            words = a_raw[:, g, t, :].bitcast(F32)
+            bank = psum.tile([P, 512], F32, name="bank", bufs=6)
+            for h in range(PASSES):
+                for u in range(2):
+                    q = 2 * h + u
+                    nc.tensor.transpose(
+                        bank[:, 128 * q : 128 * (q + 1)], words[:, 256 * h + u : 256 * (h + 1) : 2], ident[:]
+                    )
+            return bank
+
+        def copy_a(grouped, t, bank):
+            nc.scalar.copy(
+                out=grouped[:, 1024 * t : 1024 * (t + 1)].bitcast(F32).rearrange("p (h r u) -> p h r u", h=2, u=2),
+                in_=bank[:].rearrange("p (h u r) -> p h r u", h=2, u=2),
+            )
+
+        def quantize_a(grouped, g, t0, t1):
+            nc.vector.quantize_mx(
+                out=a_codes[:, g, 256 * t0 : 256 * t1].bitcast(FP8X4),
+                scales=a_scales[:, g, 256 * t0 : 256 * t1],
+                in_=grouped[:, 1024 * t0 : 1024 * t1],
+            )
+
+        def interleave_f(grouped, c, h, w0, w1, copy):
+            copy(
+                out=grouped[:, 4 * w0 : 4 * w1].rearrange("p (x i j) -> p x j i", i=4, j=4),
+                in_=f_raw[:, c, h, :, w0:w1].rearrange("p j (x i) -> p x j i", i=4),
+            )
+
+        def quantize_f(grouped, c, h):
+            nc.vector.quantize_mx(
+                out=f_codes[:, c, 512 * h : 512 * (h + 1)].bitcast(FP8X4),
+                scales=f_scales[:, c, 512 * h : 512 * (h + 1)],
+                in_=grouped[:],
+            )
+
+        def new_f_grouped():
+            grouped = stage.tile([P, 2048], BF16, name="f_grouped", bufs=3, align_bytes=64)
+            return grouped
+
+        def new_a_grouped():
+            grouped = stage.tile([P, 4096], BF16, name="a_grouped", bufs=2, align_bytes=64)
+            return grouped
+
+        def multiply(c, g, t):
+            bank = psum.tile([P, 512], F32, name="bank", bufs=6)
+            for h in range(PASSES):
+                cols = slice(256 * t + 128 * h, 256 * t + 128 * (h + 1))
+                fcols = slice(512 * h, 512 * (h + 1))
+                nc.tensor.matmul_mx(
+                    out=bank[:],
+                    lhsT=a_codes[:, g, cols].bitcast(FP8X4),
+                    lhsT_scale=a_scales[:, g, cols],
+                    rhs=f_codes[:, c, fcols].bitcast(FP8X4),
+                    rhs_scale=f_scales[:, c, fcols],
+                    start=(h == 0),
+                    stop=(h == PASSES - 1),
+                )
+            return bank
+
+        squares = {}
+        sums = {}
+        h_tiles = {}
+
+        def square(i, t, bank):
+            nc.scalar.activation(
+                out=squares[i][:, t, :].rearrange("p (d b) -> p d b", d=4),
+                in_=bank[:].rearrange("p (b d) -> p d b", d=4),
+                func=SQUARE,
+                scale=0.5,
+            )
+
+        def new_squares(i):
+            sq = stage.tile([P, TILES, 512], F32, name="sq", bufs=4, align_bytes=64)
+            squares[i] = sq
+
+        def add_one(i):
+            half = stage.tile([P, TILES, 256], F32, name="half", bufs=2, align_bytes=64)
+            nc.vector.tensor_tensor(out=half[:], in0=squares[i][:, :, 0:256], in1=squares[i][:, :, 256:512], op=ADD)
+            return half
+
+        def add_two(i, half):
+            e = stage.tile([P, TILES, P], F32, name="e", bufs=3, align_bytes=64)
+            nc.vector.tensor_tensor(out=e[:], in0=half[:, :, 0:128], in1=half[:, :, 128:256], op=ADD)
+            sums[i] = e
+
+        def cap_min(i):
+            g = i % GROUPS
+            hb = stage.tile([P, 512], BF16, name="hb", bufs=3, align_bytes=64)
+            nc.vector.tensor_tensor(
+                out=hb[:].rearrange("p (b t) -> p b t", t=TILES),
+                in0=sums[i][:].rearrange("p t b -> p b t"),
+                in1=cap_sb[:, g, :].unsqueeze(1).to_broadcast([P, P, TILES]),
+                op=MIN,
+            )
+            h_tiles[i] = hb
+
+        def quantize_h(i):
+            c, g = divmod(i, GROUPS)
+            nc.vector.quantize_mx(
+                out=h_codes[:, c, 128 * g : 128 * (g + 1)].bitcast(FP8X4),
+                scales=h_scales[:, c, 128 * g : 128 * (g + 1)],
+                in_=h_tiles[i][:],
+            )
+
+        def total_pass(dst, c, r, g):
+            nc.tensor.matmul_mx(
+                out=dst,
+                lhsT=dw[:, g, 256 * r : 256 * (r + 1)].bitcast(FP4X4),
+                lhsT_scale=dsc[:, g, 128 * r : 128 * (r + 1)],
+                rhs=h_codes[:, c, 128 * g : 128 * (g + 1)].bitcast(FP8X4),
+                rhs_scale=h_scales[:, c, 128 * g : 128 * (g + 1)],
+                start=(g == 0),
+                stop=(g == GROUPS - 1),
+            )
+
+        def totals(c, half):
+            o = psum.tile([P, 4, P], F32, name="o", bufs=2)
+            for r in range(4):
+                for g in range(GROUPS):
+                    total_pass(o[:, r, :], c, 4 * half + r, g)
+            return o
+
+        def store(o_sb, c, r0, r1):
+            dst = out[128 * r0 : 128 * r1, 128 * c : 128 * (c + 1)].rearrange("(r p) b -> p r b", p=P)
+            nc.sync.dma_start(out=dst, in_=o_sb)
+
+        def empty_totals(c, half, o):
+            o_sb = stage.tile([P, 4, P], F32, name="o_sb", bufs=2, align_bytes=64)
+            nc.scalar.copy(out=o_sb[:], in_=o[:])
+            store(o_sb[:], c, 4 * half, 4 * half + 4)
+
+        a_grouped = new_a_grouped()
+        f_grouped = [new_f_grouped(), new_f_grouped()]
+        split = 512 - F_SCALAR_COLUMNS[0]
+        for t in range(TILES):
+            copy_a(a_grouped, t, transpose_a(0, t))
+            if t < 2:
+                interleave_f(f_grouped[t], 0, t, 0, split, nc.vector.tensor_copy)
+                interleave_f(f_grouped[t], 0, t, split, 512, nc.scalar.copy)
+            quantize_a(a_grouped, 0, t, t + 1)
+            if t < 2:
+                quantize_f(f_grouped[t], 0, t)
+
+        waiting = {}
+        for i in range(UNITS):
+            c, g = divmod(i, GROUPS)
+            ahead = c == 0 and g + 1 < GROUPS
+            new_squares(i)
+
+            def turn_next():
+                grouped = new_a_grouped()
+                for t in range(TILES):
+                    copy_a(grouped, t, transpose_a(g + 1, t))
+                return grouped
+
+            if ahead and g > 0:
+                grouped_next = turn_next()
+            for t in range(TILES):
+                square(i, t, multiply(c, g, t))
+            if ahead and g == 0:
+                grouped_next = turn_next()
+
+            if c > 0 and g >= 2:
+                o = totals(c - 1, g - 2)
+                waiting[i + 1] = (c - 1, g - 2, o)
+            if i in waiting:
+                empty_totals(*waiting[i])
+
+            if c + 1 < CHUNKS and g < 2:
+                split = 512 - F_SCALAR_COLUMNS[c + 1]
+                fg = new_f_grouped()
+                f_grouped[g] = fg
+                interleave_f(fg, c + 1, g, split, 512, nc.scalar.copy)
+
+            half = None
+            if i >= 1:
+                half = add_one(i - 1)
+            if i >= 2:
+                cap_min(i - 2)
+            if i >= 1:
+                add_two(i - 1, half)
+            if i >= 2:
+                quantize_h(i - 2)
+            if ahead:
+                quantize_a(grouped_next, g + 1, 0, TILES)
+            if c + 1 < CHUNKS:
+                if g < 2:
+                    interleave_f(f_grouped[g], c + 1, g, 0, split, nc.vector.tensor_copy)
+                if g >= 1 and g < 3:
+                    quantize_f(f_grouped[g - 1], c + 1, g - 1)
+
+        last = CHUNKS - 1
+        half = add_one(UNITS - 1)
+        cap_min(UNITS - 2)
+        add_two(UNITS - 1, half)
+        quantize_h(UNITS - 2)
+        cap_min(UNITS - 1)
+        quantize_h(UNITS - 1)
+        empty_totals(*waiting[UNITS])
+        banks = []
+        for r in range(8):
+            if r < 6:
+                bank = psum.tile([P, 512], F32, name="bank", bufs=6)
+                banks.append(bank[:, 0:128])
+            else:
+                o = psum.tile([P, 4, P], F32, name="o", bufs=2)
+                banks.append(o[:, 0, :])
+        for r in range(8):
+            for g in range(GROUPS - 1):
+                total_pass(banks[r], last, r, g)
+        o_last = stage.tile([P, 8, P], F32, name="o_last", bufs=1, align_bytes=64)
+        for r in range(8):
+            total_pass(banks[r], last, r, GROUPS - 1)
+        for r in range(8):
+            copy = nc.scalar.copy if r % 2 == 0 else nc.vector.tensor_copy
+            copy(out=o_last[:, r, :], in_=banks[r])
+            if r % 4 == 3:
+                store(o_last[:, r - 3 : r + 1, :], last, r - 3, r + 1)

@@ -63,6 +63,7 @@ def tile_capped_leverage_design_totals_s13_kernel(tc, a, f, cap, d_words, d_scal
         load_a(0, 1, 2)
         load_a(0, 2, 4)
         load_a(1, 0, 4)
+        nc.sync.dma_start(out=cap_sb[:], in_=cap.rearrange("(g p t) -> p g t", g=GROUPS, t=TILES))
         load_f(1, 0)
         load_a(2, 0, 4)
         load_f(1, 1)
@@ -71,7 +72,6 @@ def tile_capped_leverage_design_totals_s13_kernel(tc, a, f, cap, d_words, d_scal
             for h in range(PASSES):
                 load_f(c, h)
         nc.sync.dma_start(out=dw[:].bitcast(I32), in_=d_words.rearrange("g p n -> p g n").bitcast(I32))
-        nc.scalar.dma_start(out=cap_sb[:], in_=cap.rearrange("(g p t) -> p g t", g=GROUPS, t=TILES))
 
         make_identity(nc, ident[:])
         nc.gpsimd.memset(dsc[:].bitcast(I32), 0)
@@ -160,10 +160,15 @@ def tile_capped_leverage_design_totals_s13_kernel(tc, a, f, cap, d_words, d_scal
             sq = stage.tile([P, TILES, 512], F32, name="sq", bufs=4, align_bytes=64)
             squares[i] = sq
 
-        def add_one(i):
-            half = stage.tile([P, TILES, 256], F32, name="half", bufs=2, align_bytes=64)
-            nc.vector.tensor_tensor(out=half[:], in0=squares[i][:, :, 0:256], in1=squares[i][:, :, 256:512], op=ADD)
+        def new_half():
+            half = stage.tile([P, TILES, 256], F32, name="half", bufs=3, align_bytes=64)
             return half
+
+        def add_one(i, half, t0, t1):
+            sq = squares[i]
+            nc.vector.tensor_tensor(
+                out=half[:, t0:t1, :], in0=sq[:, t0:t1, 0:256], in1=sq[:, t0:t1, 256:512], op=ADD
+            )
 
         def add_two(i, half):
             e = stage.tile([P, TILES, P], F32, name="e", bufs=3, align_bytes=64)
@@ -216,36 +221,37 @@ def tile_capped_leverage_design_totals_s13_kernel(tc, a, f, cap, d_words, d_scal
             nc.scalar.copy(out=o_sb[:], in_=o[:])
             store(o_sb[:], c, 4 * half, 4 * half + 4)
 
-        a_grouped = new_a_grouped()
+        a_grouped = {0: new_a_grouped()}
         f_grouped = [new_f_grouped(), new_f_grouped()]
         split = 512 - F_SCALAR_COLUMNS[0]
-        for t in range(TILES):
-            copy_a(a_grouped, t, transpose_a(0, t))
-            if t < 2:
-                interleave_f(f_grouped[t], 0, t, 0, split, nc.vector.tensor_copy)
-                interleave_f(f_grouped[t], 0, t, split, 512, nc.scalar.copy)
-            quantize_a(a_grouped, 0, t, t + 1)
-            if t < 2:
-                quantize_f(f_grouped[t], 0, t)
+        copy_a(a_grouped[0], 0, transpose_a(0, 0))
+        for h in range(PASSES):
+            interleave_f(f_grouped[h], 0, h, split, 512, nc.scalar.copy)
+        for t in range(1, TILES):
+            copy_a(a_grouped[0], t, transpose_a(0, t))
+        interleave_f(f_grouped[0], 0, 0, 0, split, nc.vector.tensor_copy)
+        quantize_a(a_grouped[0], 0, 0, 1)
+        quantize_f(f_grouped[0], 0, 0)
+        interleave_f(f_grouped[1], 0, 1, 0, split, nc.vector.tensor_copy)
+        quantize_a(a_grouped[0], 0, 1, 2)
+        quantize_f(f_grouped[1], 0, 1)
+        quantize_a(a_grouped[0], 0, 2, 3)
+        quantize_a(a_grouped[0], 0, 3, 4)
 
         waiting = {}
+        halves = {}
         for i in range(UNITS):
             c, g = divmod(i, GROUPS)
             ahead = c == 0 and g + 1 < GROUPS
             new_squares(i)
-
-            def turn_next():
-                grouped = new_a_grouped()
-                for t in range(TILES):
-                    copy_a(grouped, t, transpose_a(g + 1, t))
-                return grouped
-
-            if ahead and g > 0:
-                grouped_next = turn_next()
-            for t in range(TILES):
-                square(i, t, multiply(c, g, t))
-            if ahead and g == 0:
-                grouped_next = turn_next()
+            if ahead:
+                a_grouped[g + 1] = new_a_grouped()
+            for t0 in range(0, TILES, 2):
+                for t in range(t0, t0 + 2):
+                    square(i, t, multiply(c, g, t))
+                if ahead:
+                    for t in range(t0, t0 + 2):
+                        copy_a(a_grouped[g + 1], t, transpose_a(g + 1, t))
 
             if c > 0 and g >= 2:
                 o = totals(c - 1, g - 2)
@@ -259,17 +265,19 @@ def tile_capped_leverage_design_totals_s13_kernel(tc, a, f, cap, d_words, d_scal
                 f_grouped[g] = fg
                 interleave_f(fg, c + 1, g, split, 512, nc.scalar.copy)
 
-            half = None
             if i >= 1:
-                half = add_one(i - 1)
+                halves[i - 1] = new_half()
+                add_one(i - 1, halves[i - 1], 0, 4)
+            if ahead:
+                quantize_a(a_grouped[g + 1], g + 1, 0, 2)
             if i >= 2:
                 cap_min(i - 2)
             if i >= 1:
-                add_two(i - 1, half)
+                add_two(i - 1, halves[i - 1])
             if i >= 2:
                 quantize_h(i - 2)
             if ahead:
-                quantize_a(grouped_next, g + 1, 0, TILES)
+                quantize_a(a_grouped[g + 1], g + 1, 2, 4)
             if c + 1 < CHUNKS:
                 if g < 2:
                     interleave_f(f_grouped[g], c + 1, g, 0, split, nc.vector.tensor_copy)
@@ -277,10 +285,12 @@ def tile_capped_leverage_design_totals_s13_kernel(tc, a, f, cap, d_words, d_scal
                     quantize_f(f_grouped[g - 1], c + 1, g - 1)
 
         last = CHUNKS - 1
-        half = add_one(UNITS - 1)
+        half = new_half()
+        add_one(UNITS - 1, half, 0, 2)
         cap_min(UNITS - 2)
-        add_two(UNITS - 1, half)
+        add_one(UNITS - 1, half, 2, 4)
         quantize_h(UNITS - 2)
+        add_two(UNITS - 1, half)
         cap_min(UNITS - 1)
         quantize_h(UNITS - 1)
         empty_totals(*waiting[UNITS])
@@ -292,12 +302,11 @@ def tile_capped_leverage_design_totals_s13_kernel(tc, a, f, cap, d_words, d_scal
             else:
                 o = psum.tile([P, 4, P], F32, name="o", bufs=2)
                 banks.append(o[:, 0, :])
-        for r in range(8):
-            for g in range(GROUPS - 1):
-                total_pass(banks[r], last, r, g)
         o_last = stage.tile([P, 8, P], F32, name="o_last", bufs=1, align_bytes=64)
-        for r in range(8):
-            total_pass(banks[r], last, r, GROUPS - 1)
+        for gs in ((0, 1), (2,), (3,)):
+            for r in range(8):
+                for g in gs:
+                    total_pass(banks[r], last, r, g)
         for r in range(8):
             copy = nc.scalar.copy if r % 2 == 0 else nc.vector.tensor_copy
             copy(out=o_last[:, r, :], in_=banks[r])

@@ -23,6 +23,8 @@ GROUPS = 4
 TILES = 4
 PASSES = 2
 UNITS = CHUNKS * GROUPS
+TURN_AFTER = 1
+F_QUANT_STEPS = (1, 2)
 F_SCALAR_COLUMNS = (192, 64, 256, 256)
 
 
@@ -47,7 +49,10 @@ def tile_capped_leverage_design_totals_s13_kernel(tc, a, f, cap, d_words, d_scal
         cap_sb = keep.tile([P, GROUPS, TILES], BF16, align_bytes=64)
         warm = keep.tile([P, 2], F32, align_bytes=64)
 
+        zeros = keep.tile([P, 512], BF16, align_bytes=64)
+
         ctx.enter_context(tc.manual_schedule())
+        nc.vector.memset(zeros[:], 0.0)
 
         def load_a(g, t0, t1):
             src = a[512 * g : 512 * (g + 1), :].rearrange("(m t) k -> m t k", t=TILES)
@@ -68,9 +73,8 @@ def tile_capped_leverage_design_totals_s13_kernel(tc, a, f, cap, d_words, d_scal
         load_a(2, 0, 4)
         load_f(1, 1)
         load_a(3, 0, 4)
-        for c in (2, 3):
-            for h in range(PASSES):
-                load_f(c, h)
+        load_f(2, 0)
+        load_f(2, 1)
         nc.sync.dma_start(out=dw[:].bitcast(I32), in_=d_words.rearrange("g p n -> p g n").bitcast(I32))
 
         make_identity(nc, ident[:])
@@ -80,6 +84,8 @@ def tile_capped_leverage_design_totals_s13_kernel(tc, a, f, cap, d_words, d_scal
                 out=dsc[32 * q : 32 * q + 4, :, :].bitcast(I32),
                 in_=d_scales[:, 4 * q : 4 * q + 4, :].rearrange("g r n -> r g n").bitcast(I32),
             )
+        load_f(3, 0)
+        load_f(3, 1)
         nc.vector.memset(warm[:, 0:1], 0.0)
         nc.scalar.activation(out=warm[:, 1:2], in_=warm[:, 0:1], func=SQUARE)
 
@@ -179,9 +185,9 @@ def tile_capped_leverage_design_totals_s13_kernel(tc, a, f, cap, d_words, d_scal
             g = i % GROUPS
             hb = stage.tile([P, 512], BF16, name="hb", bufs=3, align_bytes=64)
             nc.vector.tensor_tensor(
-                out=hb[:].rearrange("p (b t) -> p b t", t=TILES),
-                in0=sums[i][:].rearrange("p t b -> p b t"),
-                in1=cap_sb[:, g, :].unsqueeze(1).to_broadcast([P, P, TILES]),
+                out=hb[:].rearrange("p (x i t) -> p x t i", i=4, t=TILES),
+                in0=sums[i][:].rearrange("p t (x i) -> p x t i", i=4),
+                in1=cap_sb[:, g, :].unsqueeze(1).unsqueeze(3).to_broadcast([P, 32, TILES, 4]),
                 op=MIN,
             )
             h_tiles[i] = hb
@@ -221,14 +227,21 @@ def tile_capped_leverage_design_totals_s13_kernel(tc, a, f, cap, d_words, d_scal
             nc.scalar.copy(out=o_sb[:], in_=o[:])
             store(o_sb[:], c, 4 * half, 4 * half + 4)
 
+        def warm_up(count):
+            bank = psum.tile([P, 512], F32, name="o", bufs=2)
+            for k in range(count):
+                nc.tensor.matmul(bank[:], zeros[:, 0:128], zeros[:], start=True, stop=True)
+
         a_grouped = {0: new_a_grouped()}
         f_grouped = [new_f_grouped(), new_f_grouped()]
         split = 512 - F_SCALAR_COLUMNS[0]
         copy_a(a_grouped[0], 0, transpose_a(0, 0))
+        warm_up(4)
         for h in range(PASSES):
             interleave_f(f_grouped[h], 0, h, split, 512, nc.scalar.copy)
         for t in range(1, TILES):
             copy_a(a_grouped[0], t, transpose_a(0, t))
+            warm_up(1)
         interleave_f(f_grouped[0], 0, 0, 0, split, nc.vector.tensor_copy)
         quantize_a(a_grouped[0], 0, 0, 1)
         quantize_f(f_grouped[0], 0, 0)
@@ -246,12 +259,11 @@ def tile_capped_leverage_design_totals_s13_kernel(tc, a, f, cap, d_words, d_scal
             new_squares(i)
             if ahead:
                 a_grouped[g + 1] = new_a_grouped()
-            for t0 in range(0, TILES, 2):
-                for t in range(t0, t0 + 2):
-                    square(i, t, multiply(c, g, t))
-                if ahead:
-                    for t in range(t0, t0 + 2):
-                        copy_a(a_grouped[g + 1], t, transpose_a(g + 1, t))
+            for t in range(TILES):
+                square(i, t, multiply(c, g, t))
+                if ahead and t == TURN_AFTER:
+                    for s in range(TILES):
+                        copy_a(a_grouped[g + 1], s, transpose_a(g + 1, s))
 
             if c > 0 and g >= 2:
                 o = totals(c - 1, g - 2)
@@ -265,32 +277,32 @@ def tile_capped_leverage_design_totals_s13_kernel(tc, a, f, cap, d_words, d_scal
                 f_grouped[g] = fg
                 interleave_f(fg, c + 1, g, split, 512, nc.scalar.copy)
 
+            halves[i] = new_half()
+            if c + 1 < CHUNKS and g < 2:
+                interleave_f(f_grouped[g], c + 1, g, 0, split, nc.vector.tensor_copy)
             if i >= 1:
-                halves[i - 1] = new_half()
-                add_one(i - 1, halves[i - 1], 0, 4)
-            if ahead:
-                quantize_a(a_grouped[g + 1], g + 1, 0, 2)
+                add_one(i - 1, halves[i - 1], 2, 4)
             if i >= 2:
                 cap_min(i - 2)
+            if ahead:
+                quantize_a(a_grouped[g + 1], g + 1, 0, 2)
             if i >= 1:
                 add_two(i - 1, halves[i - 1])
             if i >= 2:
                 quantize_h(i - 2)
+            if i == UNITS - 1:
+                cap_min(i - 1)
+            add_one(i, halves[i], 0, 2)
             if ahead:
                 quantize_a(a_grouped[g + 1], g + 1, 2, 4)
-            if c + 1 < CHUNKS:
-                if g < 2:
-                    interleave_f(f_grouped[g], c + 1, g, 0, split, nc.vector.tensor_copy)
-                if g >= 1 and g < 3:
-                    quantize_f(f_grouped[g - 1], c + 1, g - 1)
+            if c + 1 < CHUNKS and g in F_QUANT_STEPS:
+                h = F_QUANT_STEPS.index(g)
+                quantize_f(f_grouped[h], c + 1, h)
 
         last = CHUNKS - 1
-        half = new_half()
-        add_one(UNITS - 1, half, 0, 2)
-        cap_min(UNITS - 2)
-        add_one(UNITS - 1, half, 2, 4)
         quantize_h(UNITS - 2)
-        add_two(UNITS - 1, half)
+        add_one(UNITS - 1, halves[UNITS - 1], 2, 4)
+        add_two(UNITS - 1, halves[UNITS - 1])
         cap_min(UNITS - 1)
         quantize_h(UNITS - 1)
         empty_totals(*waiting[UNITS])
@@ -310,5 +322,5 @@ def tile_capped_leverage_design_totals_s13_kernel(tc, a, f, cap, d_words, d_scal
         for r in range(8):
             copy = nc.scalar.copy if r % 2 == 0 else nc.vector.tensor_copy
             copy(out=o_last[:, r, :], in_=banks[r])
-            if r % 4 == 3:
-                store(o_last[:, r - 3 : r + 1, :], last, r - 3, r + 1)
+            if r % 2 == 1:
+                store(o_last[:, r - 1 : r + 1, :], last, r - 1, r + 1)

@@ -23,9 +23,11 @@ GROUPS = 4
 TILES = 4
 PASSES = 2
 UNITS = CHUNKS * GROUPS
-TURN_AFTER = 1
+TURN_AFTER = 0
+TOTALS_STEPS = ((6, 10, 14), (7, 11, 15))
+EMPTY_STEPS = ((7, 11, 15), (8, 12, 16))
 F_QUANT_STEPS = (1, 2)
-F_SCALAR_COLUMNS = (192, 64, 256, 256)
+F_SCALAR_COLUMNS = (192, 0, 256, 256)
 
 
 def tile_capped_leverage_design_totals_s13_kernel(tc, a, f, cap, d_words, d_scales, out):
@@ -170,27 +172,34 @@ def tile_capped_leverage_design_totals_s13_kernel(tc, a, f, cap, d_words, d_scal
             half = stage.tile([P, TILES, 256], F32, name="half", bufs=3, align_bytes=64)
             return half
 
-        def add_one(i, half, t0, t1):
-            sq = squares[i]
+        def add_one(i, half, t0, t1, b0=0, b1=P):
+            sq = squares[i][:].rearrange("p t (d b) -> p t d b", d=4)
             nc.vector.tensor_tensor(
-                out=half[:, t0:t1, :], in0=sq[:, t0:t1, 0:256], in1=sq[:, t0:t1, 256:512], op=ADD
+                out=half[:].rearrange("p t (d b) -> p t d b", d=2)[:, t0:t1, :, b0:b1],
+                in0=sq[:, t0:t1, 0:2, b0:b1],
+                in1=sq[:, t0:t1, 2:4, b0:b1],
+                op=ADD,
             )
 
-        def add_two(i, half):
-            e = stage.tile([P, TILES, P], F32, name="e", bufs=3, align_bytes=64)
-            nc.vector.tensor_tensor(out=e[:], in0=half[:, :, 0:128], in1=half[:, :, 128:256], op=ADD)
-            sums[i] = e
-
-        def cap_min(i):
-            g = i % GROUPS
-            hb = stage.tile([P, 512], BF16, name="hb", bufs=3, align_bytes=64)
+        def add_two(i, half, b0=0, b1=P):
+            if b0 == 0:
+                e = stage.tile([P, TILES, P], F32, name="e", bufs=3, align_bytes=64)
+                sums[i] = e
             nc.vector.tensor_tensor(
-                out=hb[:].rearrange("p (x i t) -> p x t i", i=4, t=TILES),
-                in0=sums[i][:].rearrange("p t (x i) -> p x t i", i=4),
-                in1=cap_sb[:, g, :].unsqueeze(1).unsqueeze(3).to_broadcast([P, 32, TILES, 4]),
+                out=sums[i][:, :, b0:b1], in0=half[:, :, b0:b1], in1=half[:, :, P + b0 : P + b1], op=ADD
+            )
+
+        def cap_min(i, b0=0, b1=P):
+            g = i % GROUPS
+            if b0 == 0:
+                hb = stage.tile([P, 512], BF16, name="hb", bufs=3, align_bytes=64)
+                h_tiles[i] = hb
+            nc.vector.tensor_tensor(
+                out=h_tiles[i][:, 4 * b0 : 4 * b1].rearrange("p (x i t) -> p x t i", i=4, t=TILES),
+                in0=sums[i][:, :, b0:b1].rearrange("p t (x i) -> p x t i", i=4),
+                in1=cap_sb[:, g, :].unsqueeze(1).unsqueeze(3).to_broadcast([P, (b1 - b0) // 4, TILES, 4]),
                 op=MIN,
             )
-            h_tiles[i] = hb
 
         def quantize_h(i):
             c, g = divmod(i, GROUPS)
@@ -251,7 +260,7 @@ def tile_capped_leverage_design_totals_s13_kernel(tc, a, f, cap, d_words, d_scal
         quantize_a(a_grouped[0], 0, 2, 3)
         quantize_a(a_grouped[0], 0, 3, 4)
 
-        waiting = {}
+        waiting = []
         halves = {}
         for i in range(UNITS):
             c, g = divmod(i, GROUPS)
@@ -265,17 +274,19 @@ def tile_capped_leverage_design_totals_s13_kernel(tc, a, f, cap, d_words, d_scal
                     for s in range(TILES):
                         copy_a(a_grouped[g + 1], s, transpose_a(g + 1, s))
 
-            if c > 0 and g >= 2:
-                o = totals(c - 1, g - 2)
-                waiting[i + 1] = (c - 1, g - 2, o)
-            if i in waiting:
-                empty_totals(*waiting[i])
+            for half in range(2):
+                if i in TOTALS_STEPS[half]:
+                    done = TOTALS_STEPS[half].index(i)
+                    waiting.append((done, half, totals(done, half)))
+                if i in EMPTY_STEPS[half]:
+                    empty_totals(*waiting.pop(0))
 
             if c + 1 < CHUNKS and g < 2:
                 split = 512 - F_SCALAR_COLUMNS[c + 1]
                 fg = new_f_grouped()
                 f_grouped[g] = fg
-                interleave_f(fg, c + 1, g, split, 512, nc.scalar.copy)
+                if split < 512:
+                    interleave_f(fg, c + 1, g, split, 512, nc.scalar.copy)
 
             halves[i] = new_half()
             if c + 1 < CHUNKS and g < 2:
@@ -301,11 +312,16 @@ def tile_capped_leverage_design_totals_s13_kernel(tc, a, f, cap, d_words, d_scal
 
         last = CHUNKS - 1
         quantize_h(UNITS - 2)
-        add_one(UNITS - 1, halves[UNITS - 1], 2, 4)
-        add_two(UNITS - 1, halves[UNITS - 1])
-        cap_min(UNITS - 1)
+        parts = ((0, 64), (64, 128))
+        for b0, b1 in parts:
+            add_one(UNITS - 1, halves[UNITS - 1], 2, 4, b0, b1)
+        for b0, b1 in parts:
+            add_two(UNITS - 1, halves[UNITS - 1], b0, b1)
+        for b0, b1 in parts:
+            cap_min(UNITS - 1, b0, b1)
         quantize_h(UNITS - 1)
-        empty_totals(*waiting[UNITS])
+        while waiting:
+            empty_totals(*waiting.pop(0))
         banks = []
         for r in range(8):
             if r < 6:

@@ -250,7 +250,8 @@ def tile_capped_leverage_design_totals_s13_kernel(tc, a, f, cap, d_words, d_scal
             interleave_f(f_grouped[h], 0, h, split, 512, nc.scalar.copy)
         for t in range(1, TILES):
             copy_a(a_grouped[0], t, transpose_a(0, t))
-            warm_up(1)
+            if t == 1:
+                warm_up(1)
         interleave_f(f_grouped[0], 0, 0, 0, split, nc.vector.tensor_copy)
         quantize_a(a_grouped[0], 0, 0, 1)
         quantize_f(f_grouped[0], 0, 0)

from contextlib import ExitStack

import concourse.mybir as mybir
from concourse.masks import make_identity

F32 = mybir.dt.float32
BF16 = mybir.dt.bfloat16
U32 = mybir.dt.uint32
I32 = mybir.dt.int32
U8 = mybir.dt.uint8
FP8X4 = mybir.dt.float8_e4m3fn_x4
FP4X4 = mybir.dt.float4_e2m1fn_x4
SQUARE = mybir.ActivationFunctionType.Square
ADD = mybir.AluOpType.add
MIN = mybir.AluOpType.min

M, K, N, G, R = 2048, 1024, 2048, 512, 1024
FLOPS = 2 * M * K * N + 2 * R * M * G

P = 128
CHUNKS = 4
GROUPS = 4
TILES = 4
PASSES = 2
UNITS = CHUNKS * GROUPS
TURN_AFTER = 0
TOTALS_STEPS = ((6, 10, 14), (7, 11, 15))
EMPTY_STEPS = ((7, 11, 15), (8, 12, 16))
F_QUANT_STEPS = (1, 2)
F_SCALAR_COLUMNS = (192, 0, 256, 256)


def tile_capped_leverage_design_totals_s13_kernel(tc, a, f, cap, d_words, d_scales, out):
    nc = tc.nc
    with ExitStack() as ctx:
        keep = ctx.enter_context(tc.tile_pool(name="keep", bufs=1))
        stage = ctx.enter_context(tc.tile_pool(name="stage", bufs=2))
        psum = ctx.enter_context(tc.psum_pool(name="psum", bufs=2))

        ident = keep.tile([P, P], F32, align_bytes=64)
        a_raw = keep.tile([P, GROUPS, TILES, K], BF16, align_bytes=64)
        a_codes = keep.tile([P, GROUPS, 1024], U32, align_bytes=64)
        a_scales = keep.tile([P, GROUPS, 1024], U8, align_bytes=64)
        f_raw = keep.tile([P, CHUNKS, PASSES, 4, 512], BF16, align_bytes=64)
        f_codes = keep.tile([P, CHUNKS, 1024], U32, align_bytes=64)
        f_scales = keep.tile([P, CHUNKS, 1024], U8, align_bytes=64)
        h_codes = keep.tile([P, CHUNKS, 512], U32, align_bytes=64)
        h_scales = keep.tile([P, CHUNKS, 512], U8, align_bytes=64)
        dw = keep.tile([P, GROUPS, 2 * R], U8, align_bytes=64)
        dsc = keep.tile([P, GROUPS, R], U8, align_bytes=64)
        cap_sb = keep.tile([P, GROUPS, TILES], BF16, align_bytes=64)
        warm = keep.tile([P, 2], F32, align_bytes=64)

        zeros = keep.tile([P, 512], BF16, align_bytes=64)

        ctx.enter_context(tc.manual_schedule())
        nc.vector.memset(zeros[:], 0.0)

        def load_a(g, t0, t1):
            src = a[512 * g : 512 * (g + 1), :].rearrange("(m t) k -> m t k", t=TILES)
            nc.sync.dma_start(out=a_raw[:, g, t0:t1, :], in_=src[:, t0:t1, :])

        def load_f(c, h):
            src = f[512 * h : 512 * (h + 1), 512 * c : 512 * (c + 1)]
            nc.sync.dma_start(out=f_raw[:, c, h, :, :], in_=src.rearrange("(p j) w -> p j w", j=4))

        load_a(0, 0, 1)
        load_f(0, 0)
        load_f(0, 1)
        load_a(0, 1, 2)
        load_a(0, 2, 4)
        load_a(1, 0, 4)
        nc.sync.dma_start(out=cap_sb[:], in_=cap.rearrange("(g p t) -> p g t", g=GROUPS, t=TILES))
        load_f(1, 0)
        load_a(2, 0, 4)
        load_f(1, 1)
        load_a(3, 0, 4)
        load_f(2, 0)
        load_f(2, 1)
        nc.sync.dma_start(out=dw[:].bitcast(I32), in_=d_words.rearrange("g p n -> p g n").bitcast(I32))

        make_identity(nc, ident[:])
        nc.gpsimd.memset(dsc[:].bitcast(I32), 0)
        for q in range(4):
            nc.sync.dma_start(
                out=dsc[32 * q : 32 * q + 4, :, :].bitcast(I32),
                in_=d_scales[:, 4 * q : 4 * q + 4, :].rearrange("g r n -> r g n").bitcast(I32),
            )
        load_f(3, 0)
        load_f(3, 1)
        nc.vector.memset(warm[:, 0:1], 0.0)
        nc.scalar.activation(out=warm[:, 1:2], in_=warm[:, 0:1], func=SQUARE)

        def transpose_a(g, t):
            words = a_raw[:, g, t, :].bitcast(F32)
            bank = psum.tile([P, 512], F32, name="bank", bufs=6)
            for h in range(PASSES):
                for u in range(2):
                    q = 2 * h + u
                    nc.tensor.transpose(
                        bank[:, 128 * q : 128 * (q + 1)], words[:, 256 * h + u : 256 * (h + 1) : 2], ident[:]
                    )
            return bank

        def copy_a(grouped, t, bank):
            nc.scalar.copy(
                out=grouped[:, 1024 * t : 1024 * (t + 1)].bitcast(F32).rearrange("p (h r u) -> p h r u", h=2, u=2),
                in_=bank[:].rearrange("p (h u r) -> p h r u", h=2, u=2),
            )

        def quantize_a(grouped, g, t0, t1):
            nc.vector.quantize_mx(
                out=a_codes[:, g, 256 * t0 : 256 * t1].bitcast(FP8X4),
                scales=a_scales[:, g, 256 * t0 : 256 * t1],
                in_=grouped[:, 1024 * t0 : 1024 * t1],
            )

        def interleave_f(grouped, c, h, w0, w1, copy):
            copy(
                out=grouped[:, 4 * w0 : 4 * w1].rearrange("p (x i j) -> p x j i", i=4, j=4),
                in_=f_raw[:, c, h, :, w0:w1].rearrange("p j (x i) -> p x j i", i=4),
            )

        def quantize_f(grouped, c, h):
            nc.vector.quantize_mx(
                out=f_codes[:, c, 512 * h : 512 * (h + 1)].bitcast(FP8X4),
                scales=f_scales[:, c, 512 * h : 512 * (h + 1)],
                in_=grouped[:],
            )

        def new_f_grouped():
            grouped = stage.tile([P, 2048], BF16, name="f_grouped", bufs=3, align_bytes=64)
            return grouped

        def new_a_grouped():
            grouped = stage.tile([P, 4096], BF16, name="a_grouped", bufs=2, align_bytes=64)
            return grouped

        def multiply(c, g, t):
            bank = psum.tile([P, 512], F32, name="bank", bufs=6)
            for h in range(PASSES):
                cols = slice(256 * t + 128 * h, 256 * t + 128 * (h + 1))
                fcols = slice(512 * h, 512 * (h + 1))
                nc.tensor.matmul_mx(
                    out=bank[:],
                    lhsT=a_codes[:, g, cols].bitcast(FP8X4),
                    lhsT_scale=a_scales[:, g, cols],
                    rhs=f_codes[:, c, fcols].bitcast(FP8X4),
                    rhs_scale=f_scales[:, c, fcols],
                    start=(h == 0),
                    stop=(h == PASSES - 1),
                )
            return bank

        squares = {}
        sums = {}
        h_tiles = {}

        def square(i, t, bank):
            nc.scalar.activation(
                out=squares[i][:, t, :].rearrange("p (d b) -> p d b", d=4),
                in_=bank[:].rearrange("p (b d) -> p d b", d=4),
                func=SQUARE,
                scale=0.5,
            )

        def new_squares(i):
            sq = stage.tile([P, TILES, 512], F32, name="sq", bufs=4, align_bytes=64)
            squares[i] = sq

        def new_half():
            half = stage.tile([P, TILES, 256], F32, name="half", bufs=3, align_bytes=64)
            return half

        def add_one(i, half, t0, t1, b0=0, b1=P):
            sq = squares[i][:].rearrange("p t (d b) -> p t d b", d=4)
            nc.vector.tensor_tensor(
                out=half[:].rearrange("p t (d b) -> p t d b", d=2)[:, t0:t1, :, b0:b1],
                in0=sq[:, t0:t1, 0:2, b0:b1],
                in1=sq[:, t0:t1, 2:4, b0:b1],
                op=ADD,
            )

        def add_two(i, half, b0=0, b1=P):
            if b0 == 0:
                e = stage.tile([P, TILES, P], F32, name="e", bufs=3, align_bytes=64)
                sums[i] = e
            nc.vector.tensor_tensor(
                out=sums[i][:, :, b0:b1], in0=half[:, :, b0:b1], in1=half[:, :, P + b0 : P + b1], op=ADD
            )

        def cap_min(i, b0=0, b1=P):
            g = i % GROUPS
            if b0 == 0:
                hb = stage.tile([P, 512], BF16, name="hb", bufs=3, align_bytes=64)
                h_tiles[i] = hb
            nc.vector.tensor_tensor(
                out=h_tiles[i][:, 4 * b0 : 4 * b1].rearrange("p (x i t) -> p x t i", i=4, t=TILES),
                in0=sums[i][:, :, b0:b1].rearrange("p t (x i) -> p x t i", i=4),
                in1=cap_sb[:, g, :].unsqueeze(1).unsqueeze(3).to_broadcast([P, (b1 - b0) // 4, TILES, 4]),
                op=MIN,
            )

        def quantize_h(i):
            c, g = divmod(i, GROUPS)
            nc.vector.quantize_mx(
                out=h_codes[:, c, 128 * g : 128 * (g + 1)].bitcast(FP8X4),
                scales=h_scales[:, c, 128 * g : 128 * (g + 1)],
                in_=h_tiles[i][:],
            )

        def total_pass(dst, c, r, g):
            nc.tensor.matmul_mx(
                out=dst,
                lhsT=dw[:, g, 256 * r : 256 * (r + 1)].bitcast(FP4X4),
                lhsT_scale=dsc[:, g, 128 * r : 128 * (r + 1)],
                rhs=h_codes[:, c, 128 * g : 128 * (g + 1)].bitcast(FP8X4),
                rhs_scale=h_scales[:, c, 128 * g : 128 * (g + 1)],
                start=(g == 0),
                stop=(g == GROUPS - 1),
            )

        def totals(c, half):
            o = psum.tile([P, 4, P], F32, name="o", bufs=2)
            for r in range(4):
                for g in range(GROUPS):
                    total_pass(o[:, r, :], c, 4 * half + r, g)
            return o

        def store(o_sb, c, r0, r1):
            dst = out[128 * r0 : 128 * r1, 128 * c : 128 * (c + 1)].rearrange("(r p) b -> p r b", p=P)
            nc.sync.dma_start(out=dst, in_=o_sb)

        def empty_totals(c, half, o):
            o_sb = stage.tile([P, 4, P], F32, name="o_sb", bufs=2, align_bytes=64)
            nc.scalar.copy(out=o_sb[:], in_=o[:])
            store(o_sb[:], c, 4 * half, 4 * half + 4)

        def warm_up(count):
            bank = psum.tile([P, 512], F32, name="o", bufs=2)
            for k in range(count):
                nc.tensor.matmul(bank[:], zeros[:, 0:128], zeros[:], start=True, stop=True)

        a_grouped = {0: new_a_grouped()}
        f_grouped = [new_f_grouped(), new_f_grouped()]
        split = 512 - F_SCALAR_COLUMNS[0]
        copy_a(a_grouped[0], 0, transpose_a(0, 0))
        warm_up(4)
        for h in range(PASSES):
            interleave_f(f_grouped[h], 0, h, split, 512, nc.scalar.copy)
        for t in range(1, TILES):
            copy_a(a_grouped[0], t, transpose_a(0, t))
            if t == 1:
                warm_up(1)
        interleave_f(f_grouped[0], 0, 0, 0, split, nc.vector.tensor_copy)
        quantize_a(a_grouped[0], 0, 0, 1)
        quantize_f(f_grouped[0], 0, 0)
        interleave_f(f_grouped[1], 0, 1, 0, split, nc.vector.tensor_copy)
        quantize_a(a_grouped[0], 0, 1, 2)
        quantize_f(f_grouped[1], 0, 1)
        quantize_a(a_grouped[0], 0, 2, 3)
        quantize_a(a_grouped[0], 0, 3, 4)

        waiting = []
        halves = {}
        for i in range(UNITS):
            c, g = divmod(i, GROUPS)
            ahead = c == 0 and g + 1 < GROUPS
            new_squares(i)
            if ahead:
                a_grouped[g + 1] = new_a_grouped()
            for t in range(TILES):
                square(i, t, multiply(c, g, t))
                if ahead and t == TURN_AFTER:
                    for s in range(TILES):
                        copy_a(a_grouped[g + 1], s, transpose_a(g + 1, s))

            for half in range(2):
                if i in TOTALS_STEPS[half]:
                    done = TOTALS_STEPS[half].index(i)
                    waiting.append((done, half, totals(done, half)))
                if i in EMPTY_STEPS[half]:
                    empty_totals(*waiting.pop(0))

            if c + 1 < CHUNKS and g < 2:
                split = 512 - F_SCALAR_COLUMNS[c + 1]
                fg = new_f_grouped()
                f_grouped[g] = fg
                if split < 512:
                    interleave_f(fg, c + 1, g, split, 512, nc.scalar.copy)

            halves[i] = new_half()
            if c + 1 < CHUNKS and g < 2:
                interleave_f(f_grouped[g], c + 1, g, 0, split, nc.vector.tensor_copy)
            if i >= 1:
                add_one(i - 1, halves[i - 1], 2, 4)
            if i >= 2:
                cap_min(i - 2)
            if ahead:
                quantize_a(a_grouped[g + 1], g + 1, 0, 2)
            if i >= 1:
                add_two(i - 1, halves[i - 1])
            if i >= 2:
                quantize_h(i - 2)
            if i == UNITS - 1:
                cap_min(i - 1)
            add_one(i, halves[i], 0, 2)
            if ahead:
                quantize_a(a_grouped[g + 1], g + 1, 2, 4)
            if c + 1 < CHUNKS and g in F_QUANT_STEPS:
                h = F_QUANT_STEPS.index(g)
                quantize_f(f_grouped[h], c + 1, h)

        last = CHUNKS - 1
        quantize_h(UNITS - 2)
        parts = ((0, 64), (64, 128))
        for b0, b1 in parts:
            add_one(UNITS - 1, halves[UNITS - 1], 2, 4, b0, b1)
        for b0, b1 in parts:
            add_two(UNITS - 1, halves[UNITS - 1], b0, b1)
        for b0, b1 in parts:
            cap_min(UNITS - 1, b0, b1)
        quantize_h(UNITS - 1)
        while waiting:
            empty_totals(*waiting.pop(0))
        banks = []
        for r in range(8):
            if r < 6:
                bank = psum.tile([P, 512], F32, name="bank", bufs=6)
                banks.append(bank[:, 0:128])
            else:
                o = psum.tile([P, 4, P], F32, name="o", bufs=2)
                banks.append(o[:, 0, :])
        o_last = stage.tile([P, 8, P], F32, name="o_last", bufs=1, align_bytes=64)
        for gs in ((0, 1), (2,), (3,)):
            for r in range(8):
                for g in gs:
                    total_pass(banks[r], last, r, g)
        for r in range(8):
            copy = nc.scalar.copy if r % 2 == 0 else nc.vector.tensor_copy
            copy(out=o_last[:, r, :], in_=banks[r])
            if r % 2 == 1:
                store(o_last[:, r - 1 : r + 1, :], last, r - 1, r + 1)
